import numpy as np
import ml_dtypes

BF16 = ml_dtypes.bfloat16


def bf(x):
    return np.asarray(x, np.float32).astype(BF16)


def f32(x):
    return np.asarray(x, np.float32)


def f64(x):
    return np.asarray(x).astype(np.float64)


def striped(idx):
    return np.tile(idx.reshape(-1, 16).T, (8, 1))


S, K, H, M, N, E, Q = 512, 512, 128, 512, 128, 1, 128


def gelu_tanh(v):
    return 0.5 * v * (1.0 + np.tanh(np.sqrt(2.0 / np.pi) * (v + 0.044715 * v**3)))


def setup_inputs():
    return {"base": bf(np.random.standard_normal((M, S))), "x": bf(np.random.standard_normal((K, N))), "w": bf(np.random.standard_normal((E, K, H)) / np.sqrt(K)), "b": f32(0.5 * np.random.standard_normal((H, E))), "w2": bf(1.5 * np.random.standard_normal((E, H, M)) / np.sqrt(H)), "c": f32(0.2 + 0.8 * np.random.random_sample((1, N))), "offs": striped(np.random.permutation(S)[:N])}


def reference(base, x, w, b, w2, c, offs):
    idx = offs[:16].T.reshape(-1)
    z = f64(base).copy()
    for e in range(E):
        t = f64(w)[e].T @ f64(x)[:, e * Q : (e + 1) * Q] + f64(b)[:, e : e + 1]
        t = gelu_tanh(t) * f64(c)[:, e * Q : (e + 1) * Q]
        z[:, idx[e * Q : (e + 1) * Q]] += f64(w2)[e].T @ t
    return z

@@ -1,0 +1,67 @@
+import concourse.mybir as mybir
+from concourse.masks import make_identity
+
+BF16, F32, U16 = mybir.dt.bfloat16, mybir.dt.float32, mybir.dt.uint16
+GELU_TANH = mybir.ActivationFunctionType.Gelu_apprx_tanh
+MULT = mybir.AluOpType.mult
+
+P = 128
+S = 512
+K = 512
+M = 512
+N = 128
+K_BLOCKS = K // P
+WINDOWS = M // P
+
+FLOPS = 2 * K * P * N + 2 * P * M * N
+
+
+def tile_rows_ffnback_gelu_kernel(tc, base, x, w, b, w2, c, offs, out):
+    nc = tc.nc
+    with (
+        tc.tile_pool(name="held", bufs=1) as held,
+        tc.psum_pool(name="psum", bufs=1) as psum,
+    ):
+        offsets = held.tile([P, N // 16], U16)
+        x_sb = held.tile([P, K_BLOCKS, N], BF16)
+        w_sb = held.tile([P, K_BLOCKS, P], BF16)
+        base_sb = held.tile([P, WINDOWS, S], BF16)
+        w2_sb = held.tile([P, M], BF16)
+        bias = held.tile([P, 1], F32)
+        c_all = held.tile([P, N], F32)
+
+        nc.sync.dma_start(x_sb[:], x.rearrange("(p a) n -> p a n", a=K_BLOCKS))
+        nc.scalar.dma_start(w_sb[:], w.rearrange("e (p a) i -> p (e a) i", a=K_BLOCKS))
+        nc.sync.dma_start(base_sb[:], base.rearrange("(a p) s -> p a s", p=P))
+        nc.scalar.dma_start(w2_sb[:], w2.rearrange("e i m -> i (e m)"))
+        nc.scalar.dma_start(bias[:], b)
+        nc.sync.dma_start(offsets[:], offs)
+        nc.sync.dma_start(c_all[:], c.rearrange("o n -> (o n)").partition_broadcast(P))
+
+        ident = held.tile([P, P], BF16)
+        make_identity(nc, ident[:])
+
+        hidden = psum.tile([P, N], F32)
+        for a in range(K_BLOCKS):
+            nc.tensor.matmul(hidden[:], w_sb[:, a, :], x_sb[:, a, :], start=a == 0, stop=a == K_BLOCKS - 1)
+        gelu = held.tile([P, N], F32)
+        nc.scalar.activation(gelu[:], hidden[:], GELU_TANH, bias=bias[:])
+        h = held.tile([P, N], BF16)
+        nc.vector.tensor_tensor(h[:], gelu[:], c_all[:], MULT)
+
+        windows = [psum.tile([P, S], F32, name=f"window{m}") for m in range(WINDOWS)]
+        for m in range(WINDOWS):
+            nc.tensor.matmul(windows[m][:], ident[:], base_sb[:, m, :], start=True, stop=False)
+
+        for m in range(WINDOWS):
+            nc.tensor.matmul(
+                windows[m][:].indirect(offsets[:]), w2_sb[:, m * P : (m + 1) * P], h[:], start=False, stop=True
+            )
+
+        for m in range(WINDOWS):
+            z = held.tile([P, S], F32, name=f"z{m}")
+            if m % 2 == 0:
+                nc.vector.tensor_copy(z[:], windows[m][:])
+            else:
+                nc.scalar.copy(z[:], windows[m][:])
+            nc.sync.dma_start(out[m * P : (m + 1) * P, :], z[:])

@@ -12,6 +12,7 @@ M = 512
 N = 128
 K_BLOCKS = K // P
 WINDOWS = M // P
+WARM_UPS = 4
 
 FLOPS = 2 * K * P * N + 2 * P * M * N
 
@@ -27,23 +28,39 @@ def tile_rows_ffnback_gelu_kernel(tc, base, x, w, b, w2, c, offs, out):
         w_sb = held.tile([P, K_BLOCKS, P], BF16)
         base_sb = held.tile([P, WINDOWS, S], BF16)
         w2_sb = held.tile([P, M], BF16)
-        bias = held.tile([P, 1], F32)
+        b_row = held.tile([1, P], F32)
         c_all = held.tile([P, N], F32)
+        one = held.tile([1, 1], F32)
+        nc.vector.memset(one[:], 1.0)
 
         nc.sync.dma_start(x_sb[:], x.rearrange("(p a) n -> p a n", a=K_BLOCKS))
         nc.scalar.dma_start(w_sb[:], w.rearrange("e (p a) i -> p (e a) i", a=K_BLOCKS))
+        nc.scalar.dma_start(b_row[:], b.rearrange("i o -> o i"))
         nc.sync.dma_start(base_sb[:], base.rearrange("(a p) s -> p a s", p=P))
+        nc.scalar.dma_start(c_all[:], c.rearrange("o n -> (o n)").partition_broadcast(P))
         nc.scalar.dma_start(w2_sb[:], w2.rearrange("e i m -> i (e m)"))
-        nc.scalar.dma_start(bias[:], b)
         nc.sync.dma_start(offsets[:], offs)
-        nc.sync.dma_start(c_all[:], c.rearrange("o n -> (o n)").partition_broadcast(P))
+
+        early = held.tile([1, 1], F32)
+        nc.scalar.activation(early[:], one[:], GELU_TANH)
 
         ident = held.tile([P, P], BF16)
         make_identity(nc, ident[:])
 
+        zeros = held.tile([P, S], BF16)
+        nc.vector.memset(zeros[:], 0.0)
+        spare = psum.tile([P, S], F32)
+        for warm in range(WARM_UPS):
+            nc.tensor.matmul(spare[:], zeros[:, :P], zeros[:], start=True, stop=True)
+
         hidden = psum.tile([P, N], F32)
         for a in range(K_BLOCKS):
             nc.tensor.matmul(hidden[:], w_sb[:, a, :], x_sb[:, a, :], start=a == 0, stop=a == K_BLOCKS - 1)
+        b_column = psum.tile([P, 1], F32)
+        nc.tensor.matmul(b_column[:], b_row[:], one[:], start=True, stop=True)
+        bias = held.tile([P, 1], F32)
+        nc.vector.tensor_copy(bias[:], b_column[:])
+
         gelu = held.tile([P, N], F32)
         nc.scalar.activation(gelu[:], hidden[:], GELU_TANH, bias=bias[:])
         h = held.tile([P, N], BF16)

@@ -29,20 +29,20 @@ def tile_rows_ffnback_gelu_kernel(tc, base, x, w, b, w2, c, offs, out):
         base_sb = held.tile([P, WINDOWS, S], BF16)
         w2_sb = held.tile([P, M], BF16)
         b_row = held.tile([1, P], F32)
-        c_all = held.tile([P, N], F32)
-        one = held.tile([1, 1], F32)
-        nc.vector.memset(one[:], 1.0)
+        c_row = held.tile([1, N], F32)
+        ones = held.tile([1, P], F32)
+        nc.vector.memset(ones[:], 1.0)
 
         nc.sync.dma_start(x_sb[:], x.rearrange("(p a) n -> p a n", a=K_BLOCKS))
-        nc.scalar.dma_start(w_sb[:], w.rearrange("e (p a) i -> p (e a) i", a=K_BLOCKS))
-        nc.scalar.dma_start(b_row[:], b.rearrange("i o -> o i"))
+        nc.sync.dma_start(w_sb[:], w.rearrange("e (p a) i -> p (e a) i", a=K_BLOCKS))
+        nc.sync.dma_start(b_row[:], b.rearrange("i o -> o i"))
+        nc.sync.dma_start(c_row[:], c)
         nc.sync.dma_start(base_sb[:], base.rearrange("(a p) s -> p a s", p=P))
-        nc.scalar.dma_start(c_all[:], c.rearrange("o n -> (o n)").partition_broadcast(P))
-        nc.scalar.dma_start(w2_sb[:], w2.rearrange("e i m -> i (e m)"))
+        nc.sync.dma_start(w2_sb[:], w2.rearrange("e i m -> i (e m)"))
         nc.sync.dma_start(offsets[:], offs)
 
         early = held.tile([1, 1], F32)
-        nc.scalar.activation(early[:], one[:], GELU_TANH)
+        nc.scalar.activation(early[:], ones[:, :1], GELU_TANH)
 
         ident = held.tile([P, P], BF16)
         make_identity(nc, ident[:])
@@ -57,9 +57,11 @@ def tile_rows_ffnback_gelu_kernel(tc, base, x, w, b, w2, c, offs, out):
         for a in range(K_BLOCKS):
             nc.tensor.matmul(hidden[:], w_sb[:, a, :], x_sb[:, a, :], start=a == 0, stop=a == K_BLOCKS - 1)
         b_column = psum.tile([P, 1], F32)
-        nc.tensor.matmul(b_column[:], b_row[:], one[:], start=True, stop=True)
+        nc.tensor.matmul(b_column[:], b_row[:], ones[:, :1], start=True, stop=True)
         bias = held.tile([P, 1], F32)
         nc.vector.tensor_copy(bias[:], b_column[:])
+        c_all = psum.tile([P, N], F32)
+        nc.tensor.matmul(c_all[:], ones[:], c_row[:], start=True, stop=True)
 
         gelu = held.tile([P, N], F32)
         nc.scalar.activation(gelu[:], hidden[:], GELU_TANH, bias=bias[:])

@@ -37,7 +37,7 @@ def tile_rows_ffnback_gelu_kernel(tc, base, x, w, b, w2, c, offs, out):
         nc.sync.dma_start(w_sb[:], w.rearrange("e (p a) i -> p (e a) i", a=K_BLOCKS))
         nc.sync.dma_start(b_row[:], b.rearrange("i o -> o i"))
         nc.sync.dma_start(c_row[:], c)
-        nc.sync.dma_start(base_sb[:], base.rearrange("(a p) s -> p a s", p=P))
+        nc.sync.dma_start(base_sb[:], base.rearrange("(p a) s -> p a s", a=WINDOWS))
         nc.sync.dma_start(w2_sb[:], w2.rearrange("e i m -> i (e m)"))
         nc.sync.dma_start(offsets[:], offs)
 
@@ -74,13 +74,14 @@ def tile_rows_ffnback_gelu_kernel(tc, base, x, w, b, w2, c, offs, out):
 
         for m in range(WINDOWS):
             nc.tensor.matmul(
-                windows[m][:].indirect(offsets[:]), w2_sb[:, m * P : (m + 1) * P], h[:], start=False, stop=True
+                windows[m][:].indirect(offsets[:]), w2_sb[:, m::WINDOWS], h[:], start=False, stop=True
             )
 
+        out_rows = out.rearrange("(p a) s -> p a s", a=WINDOWS)
         for m in range(WINDOWS):
             z = held.tile([P, S], F32, name=f"z{m}")
             if m % 2 == 0:
                 nc.vector.tensor_copy(z[:], windows[m][:])
             else:
                 nc.scalar.copy(z[:], windows[m][:])
-            nc.sync.dma_start(out[m * P : (m + 1) * P, :], z[:])
+            nc.sync.dma_start(out_rows[:, m, :], z[:])

@@ -23,6 +23,8 @@ def tile_rows_ffnback_gelu_kernel(tc, base, x, w, b, w2, c, offs, out):
         tc.tile_pool(name="held", bufs=1) as held,
         tc.psum_pool(name="psum", bufs=1) as psum,
     ):
+        zeros = held.tile([P, S], BF16)
+        nc.vector.memset(zeros[:], 0.0)
         offsets = held.tile([P, N // 16], U16)
         x_sb = held.tile([P, K_BLOCKS, N], BF16)
         w_sb = held.tile([P, K_BLOCKS, P], BF16)
@@ -37,7 +39,10 @@ def tile_rows_ffnback_gelu_kernel(tc, base, x, w, b, w2, c, offs, out):
         nc.sync.dma_start(w_sb[:], w.rearrange("e (p a) i -> p (e a) i", a=K_BLOCKS))
         nc.sync.dma_start(b_row[:], b.rearrange("i o -> o i"))
         nc.sync.dma_start(c_row[:], c)
-        nc.sync.dma_start(base_sb[:], base.rearrange("(p a) s -> p a s", a=WINDOWS))
+        base_rows = base.rearrange("(p a) s -> p a s", a=WINDOWS)
+        HALF = WINDOWS // 2
+        nc.sync.dma_start(base_sb[:, :HALF, :], base_rows[:, :HALF, :])
+        nc.sync.dma_start(base_sb[:, HALF:, :], base_rows[:, HALF:, :])
         nc.sync.dma_start(w2_sb[:], w2.rearrange("e i m -> i (e m)"))
         nc.sync.dma_start(offsets[:], offs)
 
@@ -47,8 +52,6 @@ def tile_rows_ffnback_gelu_kernel(tc, base, x, w, b, w2, c, offs, out):
         ident = held.tile([P, P], BF16)
         make_identity(nc, ident[:])
 
-        zeros = held.tile([P, S], BF16)
-        nc.vector.memset(zeros[:], 0.0)
         spare = psum.tile([P, S], F32)
         for warm in range(WARM_UPS):
             nc.tensor.matmul(spare[:], zeros[:, :P], zeros[:], start=True, stop=True)

import concourse.mybir as mybir
from concourse.masks import make_identity

BF16, F32, U16 = mybir.dt.bfloat16, mybir.dt.float32, mybir.dt.uint16
GELU_TANH = mybir.ActivationFunctionType.Gelu_apprx_tanh
MULT = mybir.AluOpType.mult

P = 128
S = 512
K = 512
M = 512
N = 128
K_BLOCKS = K // P
WINDOWS = M // P
WARM_UPS = 4

FLOPS = 2 * K * P * N + 2 * P * M * N


def tile_rows_ffnback_gelu_kernel(tc, base, x, w, b, w2, c, offs, out):
    nc = tc.nc
    with (
        tc.tile_pool(name="held", bufs=1) as held,
        tc.psum_pool(name="psum", bufs=1) as psum,
    ):
        zeros = held.tile([P, S], BF16)
        nc.vector.memset(zeros[:], 0.0)
        offsets = held.tile([P, N // 16], U16)
        x_sb = held.tile([P, K_BLOCKS, N], BF16)
        w_sb = held.tile([P, K_BLOCKS, P], BF16)
        base_sb = held.tile([P, WINDOWS, S], BF16)
        w2_sb = held.tile([P, M], BF16)
        b_row = held.tile([1, P], F32)
        c_row = held.tile([1, N], F32)
        ones = held.tile([1, P], F32)
        nc.vector.memset(ones[:], 1.0)

        nc.sync.dma_start(x_sb[:], x.rearrange("(p a) n -> p a n", a=K_BLOCKS))
        nc.sync.dma_start(w_sb[:], w.rearrange("e (p a) i -> p (e a) i", a=K_BLOCKS))
        nc.sync.dma_start(b_row[:], b.rearrange("i o -> o i"))
        nc.sync.dma_start(c_row[:], c)
        base_rows = base.rearrange("(p a) s -> p a s", a=WINDOWS)
        HALF = WINDOWS // 2
        nc.sync.dma_start(base_sb[:, :HALF, :], base_rows[:, :HALF, :])
        nc.sync.dma_start(base_sb[:, HALF:, :], base_rows[:, HALF:, :])
        nc.sync.dma_start(w2_sb[:], w2.rearrange("e i m -> i (e m)"))
        nc.sync.dma_start(offsets[:], offs)

        early = held.tile([1, 1], F32)
        nc.scalar.activation(early[:], ones[:, :1], GELU_TANH)

        ident = held.tile([P, P], BF16)
        make_identity(nc, ident[:])

        spare = psum.tile([P, S], F32)
        for warm in range(WARM_UPS):
            nc.tensor.matmul(spare[:], zeros[:, :P], zeros[:], start=True, stop=True)

        hidden = psum.tile([P, N], F32)
        for a in range(K_BLOCKS):
            nc.tensor.matmul(hidden[:], w_sb[:, a, :], x_sb[:, a, :], start=a == 0, stop=a == K_BLOCKS - 1)
        b_column = psum.tile([P, 1], F32)
        nc.tensor.matmul(b_column[:], b_row[:], ones[:, :1], start=True, stop=True)
        bias = held.tile([P, 1], F32)
        nc.vector.tensor_copy(bias[:], b_column[:])
        c_all = psum.tile([P, N], F32)
        nc.tensor.matmul(c_all[:], ones[:], c_row[:], start=True, stop=True)

        gelu = held.tile([P, N], F32)
        nc.scalar.activation(gelu[:], hidden[:], GELU_TANH, bias=bias[:])
        h = held.tile([P, N], BF16)
        nc.vector.tensor_tensor(h[:], gelu[:], c_all[:], MULT)

        windows = [psum.tile([P, S], F32, name=f"window{m}") for m in range(WINDOWS)]
        for m in range(WINDOWS):
            nc.tensor.matmul(windows[m][:], ident[:], base_sb[:, m, :], start=True, stop=False)

        for m in range(WINDOWS):
            nc.tensor.matmul(
                windows[m][:].indirect(offsets[:]), w2_sb[:, m::WINDOWS], h[:], start=False, stop=True
            )

        out_rows = out.rearrange("(p a) s -> p a s", a=WINDOWS)
        for m in range(WINDOWS):
            z = held.tile([P, S], F32, name=f"z{m}")
            if m % 2 == 0:
                nc.vector.tensor_copy(z[:], windows[m][:])
            else:
                nc.scalar.copy(z[:], windows[m][:])
            nc.sync.dma_start(out_rows[:, m, :], z[:])
